import numpy as np
CORES = [19,147,275,403]
N = 4
F = 32
TK = N * F
EPS = 0.01
def setup_inputs(rng):
    return {"x": rng.standard_normal((N, 128, TK), dtype=np.float32) * (0.5 + np.abs(rng.standard_normal((1, 1, TK), dtype=np.float32)))}
def setup_inputs_big(rng):
    d = setup_inputs(rng)
    for k in ("x",): d[k] = (d[k].astype(np.float32) * 1024.0).astype(d[k].dtype)
    return d
def setup_inputs_small(rng):
    d = setup_inputs(rng)
    for k in ("x",): d[k] = (d[k].astype(np.float32) * (1 / 1024.0)).astype(d[k].dtype)
    return d
def setup_inputs_apart(rng):
    d = setup_inputs(rng)
    f = (10.0 ** rng.permutation(np.linspace(-1.5, 1.5, N))).astype(np.float32).reshape(N, 1, 1)
    for k in ("x",): d[k] = (d[k].astype(np.float32) * f).astype(d[k].dtype)
    return d
def setup_inputs_mixed(rng):
    d = setup_inputs(rng)
    f = (10.0 ** rng.uniform(-3, 3, (1, 1, TK))).astype(np.float32); shape = rng.integers(2, size=(1, 1, TK))
    for k in ("x",):
        x = d[k].astype(np.float32)
        other = x * np.where(rng.random((1, 128, TK)) < 0.5, 0.1, 1.0).astype(np.float32)
        d[k] = (np.where(shape == 1, other, x) * f).astype(d[k].dtype)
    return d
def reference(x):
    s = x.astype(np.float64).sum(axis=0)
    n = s / np.sqrt((s ** 2).sum(axis=0) / 128 + EPS)
    return {"y": np.broadcast_to(n.astype(np.float32), (N, 128, TK))}

@@ -1,0 +1,105 @@
+from concourse.bass import DstId, RemoteDMATransfer
+from concourse.mybir import AluOpType, ActivationFunctionType
+
+P = 128
+TK = 128
+H = TK // 2
+EPS = 0.01
+
+SCRATCH = {
+    "xs": ("sbuf", [P, TK], "float32"),
+    "l1": ("sbuf", [P, TK], "float32"),
+    "l2": ("sbuf", [P, TK], "float32"),
+    "s": ("sbuf", [P, TK], "float32"),
+    "sq": ("sbuf", [P, TK], "float32"),
+    "ones": ("sbuf", [P, P], "float32"),
+    "ident": ("sbuf", [P, P], "float32"),
+    "diag": ("sbuf", [P, TK], "float32"),
+    "yo": ("sbuf", [P, TK], "float32"),
+    "col": ("sbuf", [P, 32], "float32"),
+    "pp": ("psum", [P, 512], "float32"),
+    "ssp": ("psum", [P, 512], "float32"),
+    "rp": ("psum", [P, 512], "float32"),
+}
+SEMAPHORES = ["ld", "a1", "a2", "snt", "st", "c1", "cid", "vp", "vs", "asq", "tss", "aq", "av", "vr", "vb", "vc",
+              "vd", "tr", "vy"]
+
+
+def rank_program(g, core, T, topo):
+    if T.rank_of(core) is None:
+        return
+    S = T.sem
+    near = [o for o in T.cores if o != core and topo.may_write(core, o)]
+    rackn = [o for o in near if topo.rack(topo.host(o)) == topo.rack(topo.host(core))][0]
+    cablen = [o for o in near if topo.rack(topo.host(o)) != topo.rack(topo.host(core))][0]
+    both = topo.mask(core, rackn) & topo.mask(core, cablen)
+    eng = [e for e in range(16) if (both >> e) & 1]
+    m_rack = sum(1 << e for e in eng[0::2])
+    m_cable = sum(1 << e for e in eng[1::2])
+    n_rack, n_cable = len(eng[0::2]), len(eng[1::2])
+    A, B = slice(0, H), slice(H, TK)
+
+    def dst(o):
+        rid, pid = topo.addr(o, core)
+        return DstId(rid=rid, pnc=pid)
+
+    v, sc, te, sy = g.vector, g.scalar, g.tensor, g.sync
+    mult, add = AluOpType.mult, AluOpType.add
+    q, vv, r0, b, c = (T.col[:, 4 * k:4 * k + 1] for k in range(5))
+
+    sy.dma_start(T.xs[:], T.x[:]).then_inc(S.ld, 16)
+    v.memset(T.ones[:], 1.0).then_inc(S.c1, 1)
+
+    g.wait_ge(S.ld, 16)
+    g.remote_dma_fused([
+        RemoteDMATransfer(dst_ids=[dst(rackn)], dma_engine_mask=m_rack, remote_sem=S.a1,
+                          src=T.xs[:, A], dst=T.l1[:, A]),
+        RemoteDMATransfer(dst_ids=[dst(cablen)], dma_engine_mask=m_cable, remote_sem=S.a1,
+                          src=T.xs[:, B], dst=T.l1[:, B]),
+    ], local_sem=S.snt)
+    g.wait_ge(S.c1, 1)
+    g.affine_select(T.ident[:], T.ones[:], [[-1, P]], AluOpType.is_equal, 0.0, 0, 1).then_inc(S.cid, 1)
+
+    g.wait_ge(S.a1, n_rack + n_cable)
+    g.remote_dma_fused([
+        RemoteDMATransfer(dst_ids=[dst(cablen)], dma_engine_mask=m_cable, remote_sem=S.a2,
+                          srcs=[T.xs[:, A], T.l1[:, A]], dsts=[T.l2[:, A]], alu_op=1),
+        RemoteDMATransfer(dst_ids=[dst(rackn)], dma_engine_mask=m_rack, remote_sem=S.a2,
+                          srcs=[T.xs[:, B], T.l1[:, B]], dsts=[T.l2[:, B]], alu_op=1),
+    ], local_sem=S.snt)
+
+    v.wait_ge(S.ld, 16)
+    v.wait_ge(S.a1, n_rack + n_cable)
+    v.tensor_tensor(T.pp[:, 0:TK], T.xs[:], T.l1[:], add).then_inc(S.vp, 1)
+
+    v.wait_ge(S.vp, 1)
+    v.wait_ge(S.a2, n_rack + n_cable)
+    v.tensor_tensor(T.s[:], T.pp[:, 0:TK], T.l2[:], add).then_inc(S.vs, 1)
+    sc.wait_ge(S.vs, 1)
+    sc.activation(T.sq[:], T.s[:], ActivationFunctionType.Square).then_inc(S.asq, 1)
+    te.wait_ge(S.c1, 1)
+    te.wait_ge(S.asq, 1)
+    te.matmul(T.ssp[:, 0:1], T.sq[:], T.ones[:, 0:1], True, True).then_inc(S.tss, 1)
+
+    sc.wait_ge(S.tss, 1)
+    sc.activation(q, T.ssp[:, 0:1], ActivationFunctionType.Sqrt, bias=EPS, scale=1.0 / P).then_inc(S.aq, 1)
+    sc.activation(vv, T.ssp[:, 0:1], ActivationFunctionType.Identity, bias=EPS, scale=1.0 / P).then_inc(S.av, 1)
+    v.wait_ge(S.aq, 1)
+    v.reciprocal(r0, q).then_inc(S.vr, 1)
+    v.wait_ge(S.vr, 1)
+    v.wait_ge(S.av, 1)
+    v.tensor_scalar(b, vv, r0, r0, mult, mult).then_inc(S.vb, 1)
+    v.wait_ge(S.vb, 1)
+    v.tensor_scalar(c, b, -0.5, 1.5, mult, add).then_inc(S.vc, 1)
+    v.wait_ge(S.vc, 1)
+    v.wait_ge(S.cid, 1)
+    v.tensor_scalar(T.diag[:], T.ident[:], r0, c, mult, mult).then_inc(S.vd, 1)
+
+    te.wait_ge(S.vd, 1)
+    te.matmul(T.rp[:, 0:TK], T.ones[:], T.diag[:], True, True).then_inc(S.tr, 1)
+    v.wait_ge(S.tr, 1)
+    v.tensor_tensor(T.yo[:], T.s[:], T.rp[:, 0:TK], mult).then_inc(S.vy, 1)
+    sy.wait_ge(S.vy, 1)
+    sy.dma_start(T.y[:], T.yo[:]).then_inc(S.st, 16)
+    sy.wait_ge(S.st, 16)
+    g.wait_ge(S.snt, 2 * (n_rack + n_cable))

@@ -3,6 +3,7 @@ from concourse.mybir import AluOpType, ActivationFunctionType
 
 P = 128
 TK = 128
+C0 = 32
 H = TK // 2
 EPS = 0.01
 
@@ -18,11 +19,13 @@ SCRATCH = {
     "yo": ("sbuf", [P, TK], "float32"),
     "col": ("sbuf", [P, 32], "float32"),
     "pp": ("psum", [P, 512], "float32"),
-    "ssp": ("psum", [P, 512], "float32"),
-    "rp": ("psum", [P, 512], "float32"),
+    "ssx": ("psum", [P, 512], "float32"),
+    "ssy": ("psum", [P, 512], "float32"),
+    "rpa": ("psum", [P, 512], "float32"),
+    "rpb": ("psum", [P, 512], "float32"),
 }
-SEMAPHORES = ["ld", "a1", "a2", "snt", "st", "c1", "cid", "vp", "vs", "asq", "tss", "aq", "av", "vr", "vb", "vc",
-              "vd", "tr", "vy"]
+SEMAPHORES = ["ld", "a10", "a11", "a20", "a21", "snt", "sta", "stb", "c1", "cid", "vp0", "vp1", "vs0", "vs1", "asq0",
+              "vq1", "tss0", "tss1", "aq", "av", "vr", "vb", "vc", "vda", "vdb", "tra", "trb", "vya", "vyb"]
 
 
 def rank_program(g, core, T, topo):
@@ -36,8 +39,7 @@ def rank_program(g, core, T, topo):
     eng = [e for e in range(16) if (both >> e) & 1]
     m_rack = sum(1 << e for e in eng[0::2])
     m_cable = sum(1 << e for e in eng[1::2])
-    n_rack, n_cable = len(eng[0::2]), len(eng[1::2])
-    A, B = slice(0, H), slice(H, TK)
+    n_all = len(eng)
 
     def dst(o):
         rid, pid = topo.addr(o, core)
@@ -45,46 +47,68 @@ def rank_program(g, core, T, topo):
 
     v, sc, te, sy = g.vector, g.scalar, g.tensor, g.sync
     mult, add = AluOpType.mult, AluOpType.add
+    Act = ActivationFunctionType
     q, vv, r0, b, c = (T.col[:, 4 * k:4 * k + 1] for k in range(5))
+    chunks = []
+    for lo, hi in ((0, C0), (C0, TK)):
+        mid = (lo + hi) // 2
+        chunks.append((slice(lo, hi), slice(lo, mid), slice(mid, hi)))
+    arr1, arr2 = (S.a10, S.a11), (S.a20, S.a21)
 
     sy.dma_start(T.xs[:], T.x[:]).then_inc(S.ld, 16)
     v.memset(T.ones[:], 1.0).then_inc(S.c1, 1)
-
-    g.wait_ge(S.ld, 16)
-    g.remote_dma_fused([
-        RemoteDMATransfer(dst_ids=[dst(rackn)], dma_engine_mask=m_rack, remote_sem=S.a1,
-                          src=T.xs[:, A], dst=T.l1[:, A]),
-        RemoteDMATransfer(dst_ids=[dst(cablen)], dma_engine_mask=m_cable, remote_sem=S.a1,
-                          src=T.xs[:, B], dst=T.l1[:, B]),
-    ], local_sem=S.snt)
     g.wait_ge(S.c1, 1)
     g.affine_select(T.ident[:], T.ones[:], [[-1, P]], AluOpType.is_equal, 0.0, 0, 1).then_inc(S.cid, 1)
 
-    g.wait_ge(S.a1, n_rack + n_cable)
-    g.remote_dma_fused([
-        RemoteDMATransfer(dst_ids=[dst(cablen)], dma_engine_mask=m_cable, remote_sem=S.a2,
-                          srcs=[T.xs[:, A], T.l1[:, A]], dsts=[T.l2[:, A]], alu_op=1),
-        RemoteDMATransfer(dst_ids=[dst(rackn)], dma_engine_mask=m_rack, remote_sem=S.a2,
-                          srcs=[T.xs[:, B], T.l1[:, B]], dsts=[T.l2[:, B]], alu_op=1),
-    ], local_sem=S.snt)
+    g.wait_ge(S.ld, 16)
+    for k in (0, 1):
+        _, a, bb = chunks[k]
+        g.remote_dma_fused([
+            RemoteDMATransfer(dst_ids=[dst(rackn)], dma_engine_mask=m_rack, remote_sem=arr1[k],
+                              src=T.xs[:, a], dst=T.l1[:, a]),
+            RemoteDMATransfer(dst_ids=[dst(cablen)], dma_engine_mask=m_cable, remote_sem=arr1[k],
+                              src=T.xs[:, bb], dst=T.l1[:, bb]),
+        ], local_sem=S.snt)
+    for k in (0, 1):
+        _, a, bb = chunks[k]
+        g.wait_ge(arr1[k], n_all)
+        g.remote_dma_fused([
+            RemoteDMATransfer(dst_ids=[dst(cablen)], dma_engine_mask=m_cable, remote_sem=arr2[k],
+                              srcs=[T.xs[:, a], T.l1[:, a]], dsts=[T.l2[:, a]], alu_op=1),
+            RemoteDMATransfer(dst_ids=[dst(rackn)], dma_engine_mask=m_rack, remote_sem=arr2[k],
+                              srcs=[T.xs[:, bb], T.l1[:, bb]], dsts=[T.l2[:, bb]], alu_op=1),
+        ], local_sem=S.snt)
 
+    k0, k1 = chunks[0][0], chunks[1][0]
     v.wait_ge(S.ld, 16)
-    v.wait_ge(S.a1, n_rack + n_cable)
-    v.tensor_tensor(T.pp[:, 0:TK], T.xs[:], T.l1[:], add).then_inc(S.vp, 1)
+    v.wait_ge(S.a10, n_all)
+    v.tensor_tensor(T.pp[:, k0], T.xs[:, k0], T.l1[:, k0], add).then_inc(S.vp0, 1)
+    v.wait_ge(S.vp0, 1)
+    v.wait_ge(S.a20, n_all)
+    v.tensor_tensor(T.s[:, k0], T.pp[:, k0], T.l2[:, k0], add).then_inc(S.vs0, 1)
+    v.wait_ge(S.a11, n_all)
+    v.tensor_tensor(T.pp[:, k1], T.xs[:, k1], T.l1[:, k1], add).then_inc(S.vp1, 1)
+    v.wait_ge(S.vp1, 1)
+    v.wait_ge(S.a21, n_all)
+    v.tensor_tensor(T.s[:, k1], T.pp[:, k1], T.l2[:, k1], add).then_inc(S.vs1, 1)
+    v.wait_ge(S.vs1, 1)
+    v.tensor_tensor(T.sq[:, k1], T.s[:, k1], T.s[:, k1], mult).then_inc(S.vq1, 1)
 
-    v.wait_ge(S.vp, 1)
-    v.wait_ge(S.a2, n_rack + n_cable)
-    v.tensor_tensor(T.s[:], T.pp[:, 0:TK], T.l2[:], add).then_inc(S.vs, 1)
-    sc.wait_ge(S.vs, 1)
-    sc.activation(T.sq[:], T.s[:], ActivationFunctionType.Square).then_inc(S.asq, 1)
+    sc.wait_ge(S.vs0, 1)
+    sc.activation(T.sq[:, k0], T.s[:, k0], Act.Square).then_inc(S.asq0, 1)
     te.wait_ge(S.c1, 1)
-    te.wait_ge(S.asq, 1)
-    te.matmul(T.ssp[:, 0:1], T.sq[:], T.ones[:, 0:1], True, True).then_inc(S.tss, 1)
+    te.wait_ge(S.asq0, 1)
+    te.matmul(T.ssx[0:C0, 0:1], T.sq[:, k0], T.ones[:, 0:1], True, True).then_inc(S.tss0, 1)
+    sc.wait_ge(S.tss0, 1)
+    sc.activation(T.col[0:C0, 0:1], T.ssx[0:C0, 0:1], Act.Sqrt, bias=EPS, scale=1.0 / P).then_inc(S.aq, 1)
+    te.wait_ge(S.vq1, 1)
+    te.matmul(T.ssy[:, 0:1], T.sq[:], T.ones[:, 0:1], True, True).then_inc(S.tss1, 1)
+    sc.wait_ge(S.tss1, 1)
+    for lo, hi in ((C0, H), (H, TK)):
+        sc.activation(T.col[lo:hi, 0:1], T.ssy[lo:hi, 0:1], Act.Sqrt, bias=EPS, scale=1.0 / P).then_inc(S.aq, 1)
+    sc.activation(vv, T.ssy[:, 0:1], Act.Identity, bias=EPS, scale=1.0 / P).then_inc(S.av, 1)
 
-    sc.wait_ge(S.tss, 1)
-    sc.activation(q, T.ssp[:, 0:1], ActivationFunctionType.Sqrt, bias=EPS, scale=1.0 / P).then_inc(S.aq, 1)
-    sc.activation(vv, T.ssp[:, 0:1], ActivationFunctionType.Identity, bias=EPS, scale=1.0 / P).then_inc(S.av, 1)
-    v.wait_ge(S.aq, 1)
+    v.wait_ge(S.aq, 3)
     v.reciprocal(r0, q).then_inc(S.vr, 1)
     v.wait_ge(S.vr, 1)
     v.wait_ge(S.av, 1)
@@ -93,13 +117,22 @@ def rank_program(g, core, T, topo):
     v.tensor_scalar(c, b, -0.5, 1.5, mult, add).then_inc(S.vc, 1)
     v.wait_ge(S.vc, 1)
     v.wait_ge(S.cid, 1)
-    v.tensor_scalar(T.diag[:], T.ident[:], r0, c, mult, mult).then_inc(S.vd, 1)
 
-    te.wait_ge(S.vd, 1)
-    te.matmul(T.rp[:, 0:TK], T.ones[:], T.diag[:], True, True).then_inc(S.tr, 1)
-    v.wait_ge(S.tr, 1)
-    v.tensor_tensor(T.yo[:], T.s[:], T.rp[:, 0:TK], mult).then_inc(S.vy, 1)
-    sy.wait_ge(S.vy, 1)
-    sy.dma_start(T.y[:], T.yo[:]).then_inc(S.st, 16)
-    sy.wait_ge(S.st, 16)
-    g.wait_ge(S.snt, 2 * (n_rack + n_cable))
+    ha, hb = slice(0, H), slice(H, TK)
+    v.tensor_scalar(T.diag[:, ha], T.ident[:, ha], r0, c, mult, mult).then_inc(S.vda, 1)
+    v.tensor_scalar(T.diag[:, hb], T.ident[:, hb], r0, c, mult, mult).then_inc(S.vdb, 1)
+    te.wait_ge(S.vda, 1)
+    te.matmul(T.rpa[:, 0:H], T.ones[:], T.diag[:, ha], True, True).then_inc(S.tra, 1)
+    te.wait_ge(S.vdb, 1)
+    te.matmul(T.rpb[:, 0:H], T.ones[:], T.diag[:, hb], True, True).then_inc(S.trb, 1)
+    v.wait_ge(S.tra, 1)
+    v.tensor_tensor(T.yo[:, ha], T.s[:, ha], T.rpa[:, 0:H], mult).then_inc(S.vya, 1)
+    v.wait_ge(S.trb, 1)
+    v.tensor_tensor(T.yo[:, hb], T.s[:, hb], T.rpb[:, 0:H], mult).then_inc(S.vyb, 1)
+    sy.wait_ge(S.vya, 1)
+    sy.dma_start(T.y[:, ha], T.yo[:, ha]).then_inc(S.sta, 16)
+    sc.wait_ge(S.vyb, 1)
+    sc.dma_start(T.y[:, hb], T.yo[:, hb]).then_inc(S.stb, 16)
+    sy.wait_ge(S.sta, 16)
+    sc.wait_ge(S.stb, 16)
+    g.wait_ge(S.snt, 4 * n_all)

from concourse.bass import DstId, RemoteDMATransfer
from concourse.mybir import AluOpType, ActivationFunctionType

P = 128
TK = 128
C0 = 32
H = TK // 2
EPS = 0.01

SCRATCH = {
    "xs": ("sbuf", [P, TK], "float32"),
    "l1": ("sbuf", [P, TK], "float32"),
    "l2": ("sbuf", [P, TK], "float32"),
    "s": ("sbuf", [P, TK], "float32"),
    "sq": ("sbuf", [P, TK], "float32"),
    "ones": ("sbuf", [P, P], "float32"),
    "ident": ("sbuf", [P, P], "float32"),
    "diag": ("sbuf", [P, TK], "float32"),
    "yo": ("sbuf", [P, TK], "float32"),
    "col": ("sbuf", [P, 32], "float32"),
    "pp": ("psum", [P, 512], "float32"),
    "ssx": ("psum", [P, 512], "float32"),
    "ssy": ("psum", [P, 512], "float32"),
    "rpa": ("psum", [P, 512], "float32"),
    "rpb": ("psum", [P, 512], "float32"),
}
SEMAPHORES = ["ld", "a10", "a11", "a20", "a21", "snt", "sta", "stb", "c1", "cid", "vp0", "vp1", "vs0", "vs1", "asq0",
              "vq1", "tss0", "tss1", "aq", "av", "vr", "vb", "vc", "vda", "vdb", "tra", "trb", "vya", "vyb"]


def rank_program(g, core, T, topo):
    if T.rank_of(core) is None:
        return
    S = T.sem
    near = [o for o in T.cores if o != core and topo.may_write(core, o)]
    rackn = [o for o in near if topo.rack(topo.host(o)) == topo.rack(topo.host(core))][0]
    cablen = [o for o in near if topo.rack(topo.host(o)) != topo.rack(topo.host(core))][0]
    both = topo.mask(core, rackn) & topo.mask(core, cablen)
    eng = [e for e in range(16) if (both >> e) & 1]
    m_rack = sum(1 << e for e in eng[0::2])
    m_cable = sum(1 << e for e in eng[1::2])
    n_all = len(eng)

    def dst(o):
        rid, pid = topo.addr(o, core)
        return DstId(rid=rid, pnc=pid)

    v, sc, te, sy = g.vector, g.scalar, g.tensor, g.sync
    mult, add = AluOpType.mult, AluOpType.add
    Act = ActivationFunctionType
    q, vv, r0, b, c = (T.col[:, 4 * k:4 * k + 1] for k in range(5))
    chunks = []
    for lo, hi in ((0, C0), (C0, TK)):
        mid = (lo + hi) // 2
        chunks.append((slice(lo, hi), slice(lo, mid), slice(mid, hi)))
    arr1, arr2 = (S.a10, S.a11), (S.a20, S.a21)

    sy.dma_start(T.xs[:], T.x[:]).then_inc(S.ld, 16)
    v.memset(T.ones[:], 1.0).then_inc(S.c1, 1)
    g.wait_ge(S.c1, 1)
    g.affine_select(T.ident[:], T.ones[:], [[-1, P]], AluOpType.is_equal, 0.0, 0, 1).then_inc(S.cid, 1)

    g.wait_ge(S.ld, 16)
    for k in (0, 1):
        _, a, bb = chunks[k]
        g.remote_dma_fused([
            RemoteDMATransfer(dst_ids=[dst(rackn)], dma_engine_mask=m_rack, remote_sem=arr1[k],
                              src=T.xs[:, a], dst=T.l1[:, a]),
            RemoteDMATransfer(dst_ids=[dst(cablen)], dma_engine_mask=m_cable, remote_sem=arr1[k],
                              src=T.xs[:, bb], dst=T.l1[:, bb]),
        ], local_sem=S.snt)
    for k in (0, 1):
        _, a, bb = chunks[k]
        g.wait_ge(arr1[k], n_all)
        g.remote_dma_fused([
            RemoteDMATransfer(dst_ids=[dst(cablen)], dma_engine_mask=m_cable, remote_sem=arr2[k],
                              srcs=[T.xs[:, a], T.l1[:, a]], dsts=[T.l2[:, a]], alu_op=1),
            RemoteDMATransfer(dst_ids=[dst(rackn)], dma_engine_mask=m_rack, remote_sem=arr2[k],
                              srcs=[T.xs[:, bb], T.l1[:, bb]], dsts=[T.l2[:, bb]], alu_op=1),
        ], local_sem=S.snt)

    k0, k1 = chunks[0][0], chunks[1][0]
    v.wait_ge(S.ld, 16)
    v.wait_ge(S.a10, n_all)
    v.tensor_tensor(T.pp[:, k0], T.xs[:, k0], T.l1[:, k0], add).then_inc(S.vp0, 1)
    v.wait_ge(S.vp0, 1)
    v.wait_ge(S.a20, n_all)
    v.tensor_tensor(T.s[:, k0], T.pp[:, k0], T.l2[:, k0], add).then_inc(S.vs0, 1)
    v.wait_ge(S.a11, n_all)
    v.tensor_tensor(T.pp[:, k1], T.xs[:, k1], T.l1[:, k1], add).then_inc(S.vp1, 1)
    v.wait_ge(S.vp1, 1)
    v.wait_ge(S.a21, n_all)
    v.tensor_tensor(T.s[:, k1], T.pp[:, k1], T.l2[:, k1], add).then_inc(S.vs1, 1)
    v.wait_ge(S.vs1, 1)
    v.tensor_tensor(T.sq[:, k1], T.s[:, k1], T.s[:, k1], mult).then_inc(S.vq1, 1)

    sc.wait_ge(S.vs0, 1)
    sc.activation(T.sq[:, k0], T.s[:, k0], Act.Square).then_inc(S.asq0, 1)
    te.wait_ge(S.c1, 1)
    te.wait_ge(S.asq0, 1)
    te.matmul(T.ssx[0:C0, 0:1], T.sq[:, k0], T.ones[:, 0:1], True, True).then_inc(S.tss0, 1)
    sc.wait_ge(S.tss0, 1)
    sc.activation(T.col[0:C0, 0:1], T.ssx[0:C0, 0:1], Act.Sqrt, bias=EPS, scale=1.0 / P).then_inc(S.aq, 1)
    te.wait_ge(S.vq1, 1)
    te.matmul(T.ssy[:, 0:1], T.sq[:], T.ones[:, 0:1], True, True).then_inc(S.tss1, 1)
    sc.wait_ge(S.tss1, 1)
    for lo, hi in ((C0, H), (H, TK)):
        sc.activation(T.col[lo:hi, 0:1], T.ssy[lo:hi, 0:1], Act.Sqrt, bias=EPS, scale=1.0 / P).then_inc(S.aq, 1)
    sc.activation(vv, T.ssy[:, 0:1], Act.Identity, bias=EPS, scale=1.0 / P).then_inc(S.av, 1)

    v.wait_ge(S.aq, 3)
    v.reciprocal(r0, q).then_inc(S.vr, 1)
    v.wait_ge(S.vr, 1)
    v.wait_ge(S.av, 1)
    v.tensor_scalar(b, vv, r0, r0, mult, mult).then_inc(S.vb, 1)
    v.wait_ge(S.vb, 1)
    v.tensor_scalar(c, b, -0.5, 1.5, mult, add).then_inc(S.vc, 1)
    v.wait_ge(S.vc, 1)
    v.wait_ge(S.cid, 1)

    ha, hb = slice(0, H), slice(H, TK)
    v.tensor_scalar(T.diag[:, ha], T.ident[:, ha], r0, c, mult, mult).then_inc(S.vda, 1)
    v.tensor_scalar(T.diag[:, hb], T.ident[:, hb], r0, c, mult, mult).then_inc(S.vdb, 1)
    te.wait_ge(S.vda, 1)
    te.matmul(T.rpa[:, 0:H], T.ones[:], T.diag[:, ha], True, True).then_inc(S.tra, 1)
    te.wait_ge(S.vdb, 1)
    te.matmul(T.rpb[:, 0:H], T.ones[:], T.diag[:, hb], True, True).then_inc(S.trb, 1)
    v.wait_ge(S.tra, 1)
    v.tensor_tensor(T.yo[:, ha], T.s[:, ha], T.rpa[:, 0:H], mult).then_inc(S.vya, 1)
    v.wait_ge(S.trb, 1)
    v.tensor_tensor(T.yo[:, hb], T.s[:, hb], T.rpb[:, 0:H], mult).then_inc(S.vyb, 1)
    sy.wait_ge(S.vya, 1)
    sy.dma_start(T.y[:, ha], T.yo[:, ha]).then_inc(S.sta, 16)
    sc.wait_ge(S.vyb, 1)
    sc.dma_start(T.y[:, hb], T.yo[:, hb]).then_inc(S.stb, 16)
    sy.wait_ge(S.sta, 16)
    sc.wait_ge(S.stb, 16)
    g.wait_ge(S.snt, 4 * n_all)
